import numpy as np
CORES = [33,38,57,62,81,86,161,166,185,190,209,214]
N = 12
J, Q = 1024, 4096
def entries(a): return a.T.reshape(-1)
def pack(v, P): return np.ascontiguousarray(np.asarray(v, np.int32).reshape(-1, P).T)
def split(rng, total, parts):
    c = np.sort(rng.integers(0, total + 1, parts - 1)); return np.diff(np.concatenate([[0], c, [total]]))
def lists(rng, how):
    s = np.concatenate([[0], rng.integers(1 - Q // 2, Q // 2 + 1, N - 1), [int(rng.integers(1 - Q // 2, 1))]])
    if how == "early": s[1:] = -Q; s[N] = -2 * Q
    if how == "late": s[1:] = Q; s[N] = 0
    if how == "long":
        z = int(rng.integers(1, N - 1)); s[1:z] = -rng.integers(1, Q, z - 1); s[z] = -Q; s[z + 1] = Q; s[z + 2:N] = rng.integers(1, Q, N - z - 2); s[N] = -int(rng.integers(0, Q - s[N - 1] + 1))
    if how == "sway":
        z = int(rng.integers(1, N - 2)); e = int(rng.integers(z + 1, N - 1)); s[1:] = -rng.integers(Q // 2 + 1, Q, N); s[z + 1:e + 1] = rng.integers(Q // 2 + 1, Q - 1, e - z); s[e + 1] = s[e] - Q; s[N] = s[N - 1] - Q + int(rng.integers(1, -s[N - 1]))
    tot = Q + np.diff(s)
    L = np.stack([split(rng, int(t), J) for t in tot])
    if how == "gaps":
        L = np.zeros((N, J), np.int64)
        for r in range(N): m = 1 if r & 1 else 8; L[r, 1 + rng.permutation(J - 2)[:m]] = split(rng, int(tot[r]), m)
    if how == "long":
        L = np.zeros((N, J), np.int64); L[np.arange(N), rng.integers(0, J, N)] = tot
    return {"ln": np.stack([pack(l, 16) for l in L])}
def setup_inputs(rng):
    return dict({"x": rng.standard_normal((N, 128, J), dtype=np.float32)}, **lists(rng, "uniform"))
def setup_inputs_early(rng):
    d = setup_inputs(rng); d.update(lists(rng, "early"))
    for k in ("x",): d[k] = (d[k].astype(np.float32) * 1048576.0).astype(d[k].dtype)
    return d
def setup_inputs_gaps(rng):
    d = setup_inputs(rng); d.update(lists(rng, "gaps"))
    for k in ("x",): d[k] = (d[k].astype(np.float32) * (1 / 1024.0)).astype(d[k].dtype)
    return d
def setup_inputs_late(rng):
    d = setup_inputs(rng); d.update(lists(rng, "late"))
    return d
def setup_inputs_long(rng):
    d = setup_inputs(rng); d.update(lists(rng, "long"))
    return d
def setup_inputs_sway(rng):
    d = setup_inputs(rng); d.update(lists(rng, "sway"))
    return d
def check_inputs(x):
    bad = []
    if x["ln"].min() < 0 or x["ln"].max() >= N * Q + 1: bad.append("ln out of range")
    if int(x["ln"].sum()) > N * Q: bad.append("the lengths come to more than N * Q")
    c = np.concatenate([[0], np.cumsum([int(a.sum()) for a in x["ln"]])])
    if any(c[r] < (r - 1) * Q or c[r + 1] > (r + 2) * Q for r in range(N)): bad.append("the sums of the lengths before or up to a rank leave their bounds")
    return bad
def reference(x, ln):
    got = np.concatenate([np.repeat(x[r], entries(ln[r]), axis=1) for r in range(N)], axis=1)[:, :N * Q]
    Y = np.zeros((128, N * Q), x.dtype); Y[:, :got.shape[1]] = got
    return {"y": np.stack([Y[:, Q * r:Q * r + Q] for r in range(N)])}

@@ -1,0 +1,353 @@
+from concourse.bass import DstId, RemoteDMATransfer
+from concourse.mybir import AluOpType, AxisListType, ActivationFunctionType
+
+N, J, Q, CORES_ALL = 12, 1024, 4096, 256
+SC = 256.0
+MAGIC = 1.5 * 2.0 ** 35
+
+SCRATCH = {
+    "dln": ("dram", [128, 8], "int32"),
+    "hp": ("dram", [128, 8], "int32"),
+    "far": ("dram", [10, 128, 8], "int32"),
+    "L": ("sbuf", [128, 24], "int32"),
+    "Lf": ("sbuf", [128, 24], "float32"),
+    "FL": ("sbuf", [128, 80], "int32"),
+    "FLf": ("sbuf", [128, 80], "float32"),
+    "fr": ("sbuf", [128, 4], "float32"),
+    "S": ("sbuf", [128, 32], "float32"),
+    "win": ("sbuf", [128, 3076], "float32"),
+    "hb": ("sbuf", [128, 512], "float32"),
+    "yb": ("sbuf", [128, 4096], "float32"),
+    "c256": ("sbuf", [128, 256], "int32"),
+    "kk": ("sbuf", [128, 4], "int32"),
+    "k7": ("sbuf", [128, 4], "int32"),
+    "k8": ("sbuf", [128, 4], "int32"),
+    "m7": ("sbuf", [128, 128], "int32"),
+    "m8": ("sbuf", [128, 128], "int32"),
+    "m15": ("sbuf", [128, 128], "int32"),
+    "kf": ("sbuf", [128, 4], "float32"),
+    "Meq": ("sbuf", [128, 128], "float32"),
+    "Mlt": ("sbuf", [128, 128], "float32"),
+    "Mgt": ("sbuf", [128, 128], "float32"),
+    "M3a": ("sbuf", [128, 128], "float32"),
+    "M3": ("sbuf", [128, 128], "float32"),
+    "Mone": ("sbuf", [128, 128], "float32"),
+    "ihi": ("sbuf", [128, 256], "bfloat16"),
+    "ilo": ("sbuf", [128, 128], "bfloat16"),
+    "ones": ("sbuf", [128, 256], "bfloat16"),
+    "I16": ("sbuf", [128, 128], "float16"),
+    "S2": ("sbuf", [128, 128], "float16"),
+    "rhs": ("sbuf", [128, 24 * 256], "bfloat16"),
+    "lhs": ("sbuf", [128, 24 * 128], "bfloat16"),
+    "Xn": ("sbuf", [128, 24], "float32"),
+    "X": ("sbuf", [128, 24], "float32"),
+    "hi": ("sbuf", [128, 24], "float32"),
+    "dd": ("sbuf", [128, 24], "float32"),
+    "Cn": ("sbuf", [128, 4], "float32"),
+    "Sca": ("sbuf", [128, 264], "float16"),
+    "offs": ("sbuf", [128, 256], "uint16"),
+    "psP": ("psum", [128, 512], "float32"),
+    "psB": ("psum", [128, 512], "float32"),
+    "psF": ("psum", [128, 512], "float32"),
+    "psA": ("psum", [128, 512], "float32"),
+    "psI": ("psum", [128, 512], "float32"),
+}
+SEMAPHORES = ["lnd", "lns", "xa", "xb", "near", "hpl", "farm", "fl", "xl", "hx0", "hx1", "ls", "gi", "v", "s", "pe",
+              "sty", "sts"]
+
+
+def split(mask, n):
+    bits = [1 << b for b in range(16) if mask >> b & 1]
+    k = len(bits) // n
+    return [sum(bits[i * k:(i + 1) * k]) for i in range(n)]
+
+
+def pop(mask):
+    return bin(mask).count("1")
+
+
+def helpers(q, T, topo):
+    c, d = T.cores[q], T.cores[q - 1]
+    got = [h for h in range(CORES_ALL) if topo.host(h) == topo.host(c) and topo.chip(h) == topo.chip(c)
+           and topo.die(h) == topo.die(c) and T.rank_of(h) is None and topo.may_write(h, d)]
+    return got[:2]
+
+
+def list_calls(q, T, topo):
+    c = T.cores[q]
+    if q % 2 == 0:
+        a, b = split(topo.mask(c, T.cores[q + 1]), 2)
+        return [[("dln", [q + 1], ("hp", 0), a), ("dln", [q + 1], ("L", 0), b)], []]
+    on = topo.mask(c, T.cores[q - 1])
+    first, second = [], []
+    mine, his = list(range(q + 2, N)), list(range(q + 1, N))
+    if q + 1 < N:
+        off = topo.mask(c, T.cores[q + 1])
+        parts = split(off, 2) if mine else [off]
+        first.append(("dln", [q + 1], ("L", 0), parts[0]))
+        if mine:
+            first.append(("dln", mine, ("far", q), parts[1]))
+        first.append(("dln", [q - 1], ("L", 16), on & ~off))
+    else:
+        first.append(("dln", [q - 1], ("L", 16), on))
+    off = topo.mask(c, T.cores[q + 1] if q + 1 < N else T.cores[q - 2])
+    parts = split(off, 2) if (his and q >= 3) else [off, off]
+    if his:
+        second.append(("hp", his, ("far", q - 1), parts[0]))
+    if q >= 3:
+        second.append(("hp", [q - 2], ("L", 16), parts[1]))
+    return [first, second]
+
+
+def x_calls(q, T, topo):
+    c = T.cores[q]
+    h = J // 2
+    mate = q + 1 if q % 2 == 0 else q - 1
+    other = q - 1 if q % 2 == 0 else q + 1
+    on = topo.mask(c, T.cores[mate])
+
+    def to(d, s0, w, m):
+        return (T.cores[d], "win", (q - d + 1) * J + s0, s0, w, m, "xl")
+    if not 0 <= other < N:
+        return [(h, [to(mate, 0, h, on)]), (J, [to(mate, h, h, on)])]
+    if topo.may_write(c, T.cores[other]):
+        off = topo.mask(c, T.cores[other])
+        return [(s + h, [to(other, s, h, off), to(mate, s, h, on & ~off)]) for s in (0, h)]
+    hs = helpers(q, T, topo)
+    w = h // 2
+    masks = split(topo.mask(c, hs[0]) & topo.mask(c, hs[1]), 2)
+    calls = [((a + 1) * h, [(hs[i], "hb", a * w, a * h + i * w, w, masks[i], "hx%d" % a) for i in (0, 1)])
+             for a in (0, 1)]
+    return calls + [(J, [to(mate, 0, J, on)])]
+
+
+def rank_program(g, core, T, topo):
+    rank = T.rank_of(core)
+    sem = T.sem
+    sent = [0]
+
+    def fused(transfers):
+        out = []
+        for src, dsts, mask, rsem in transfers:
+            ids = []
+            for d, ap in dsts:
+                rid, pid = topo.addr(d, core)
+                ids.append(DstId(rid=rid, pnc=pid))
+            out.append(RemoteDMATransfer(dst_ids=ids, dma_engine_mask=mask, remote_sem=rsem, srcs=[src],
+                                         dsts=[ap for d, ap in dsts]))
+            sent[0] += pop(mask)
+        g.remote_dma_fused(out, local_sem=sem.ls)
+
+    if rank is None:
+        for q in range(2, N, 2):
+            if topo.may_write(T.cores[q], T.cores[q - 1]):
+                continue
+            hs = helpers(q, T, topo)
+            if core not in hs:
+                continue
+            i, d, w = hs.index(core), T.cores[q - 1], J // 4
+            for a in (0, 1):
+                inc = pop(split(topo.mask(T.cores[q], hs[0]) & topo.mask(T.cores[q], hs[1]), 2)[i])
+                g.wait_ge(sem["hx%d" % a], inc)
+                c0 = 2 * J + a * (J // 2) + i * w
+                fused([(T.hb[:, a * w:(a + 1) * w], [(d, T.win[:, c0:c0 + w])], topo.mask(core, d), sem.xl)])
+            g.wait_ge(sem.ls, sent[0])
+        return
+
+    r = rank
+    n_near = n_far = n_hp = n_x = 0
+    for q in range(N):
+        for call in list_calls(q, T, topo):
+            for src, dsts, place, mask in call:
+                if r in dsts:
+                    n_near += pop(mask) if place[0] == "L" else 0
+                    n_far += pop(mask) if place[0] == "far" else 0
+                    n_hp += pop(mask) if place[0] == "hp" else 0
+        if q == r:
+            continue
+        for need, call in x_calls(q, T, topo):
+            for dst, buf, d0, s0, w, mask, sname in call:
+                if dst == core:
+                    n_x += pop(mask)
+        if q == r + 1 and q % 2 == 0 and not topo.may_write(T.cores[q], core):
+            n_x += sum(2 * pop(topo.mask(h, core)) for h in helpers(q, T, topo))
+
+    first, last = (1 if r == 0 else 0), (1 if r == N - 1 else 2)
+    nl = last - first + 1
+    nt = 8 * nl
+    w0, w1 = first * J, (last + 1) * J
+    zeros = r >= N - 2
+    V, S, P, Y = g.vector, g.scalar, g.tensor, g.sync
+    A = AluOpType
+    nfar = max(0, r - 1)
+
+    h = J // 2
+    Y.dma_start(T.dln[:], T.ln[:]).then_inc(sem.lnd, 16)
+    S.dma_start(T.L[:, 8:16], T.ln[:]).then_inc(sem.lns, 16)
+    Y.dma_start(T.win[:, J:J + h], T.x[:, 0:h]).then_inc(sem.xa, 16)
+    S.dma_start(T.win[:, J + h:2 * J], T.x[:, h:J]).then_inc(sem.xb, 16)
+
+    g.iota(T.c256[:], [[1, 256]], 0, 0).then_inc(sem.gi, 1)
+    g.iota(T.kk[:, 0:1], [[1, 1]], 0, 1).then_inc(sem.gi, 1)
+    g.wait_ge(sem.lnd, 16)
+    for k, call in enumerate(list_calls(r, T, topo)):
+        if not call:
+            continue
+        if k == 1:
+            g.wait_ge(sem.hpl, n_hp)
+        trs = []
+        for src, dsts, place, mask in call:
+            if place[0] == "L":
+                ap, rs = T.L[:, place[1]:place[1] + 8], sem.near
+            elif place[0] == "far":
+                ap, rs = T.far[place[1]], sem.farm
+            else:
+                ap, rs = T.hp[:], sem.hpl
+            trs.append((T[src][:], [(T.cores[d], ap) for d in dsts], mask, rs))
+        fused(trs)
+    for need, call in x_calls(r, T, topo):
+        g.wait_ge(sem.xa, 16)
+        if need > h:
+            g.wait_ge(sem.xb, 16)
+        fused([(T.win[:, J + s0:J + s0 + w], [(dst, T[buf][:, d0:d0 + w])], mask, sem[sname])
+               for dst, buf, d0, s0, w, mask, sname in call])
+
+    nv, ns, npe = [0], [0], [0]
+
+    def v(ins):
+        ins.then_inc(sem.v, 1)
+        nv[0] += 1
+        return nv[0]
+
+    def s(ins):
+        ins.then_inc(sem.s, 1)
+        ns[0] += 1
+        return ns[0]
+
+    def pe(ins):
+        ins.then_inc(sem.pe, 1)
+        npe[0] += 1
+        return npe[0]
+
+    def vw(n):
+        V.wait_ge(sem.v, n)
+
+    V.wait_ge(sem.gi, 2)
+    v(V.tensor_scalar(T.ihi[:], T.c256[:], 16.0 * SC, None, A.mult))
+    a_ihi = nv[0]
+    v(V.tensor_scalar(T.k7[:, 0:1], T.kk[:, 0:1], 7, None, A.bitwise_and))
+    v(V.tensor_scalar(T.k8[:, 0:1], T.kk[:, 0:1], 3, None, A.arith_shift_right))
+    v(V.tensor_scalar(T.m7[:], T.c256[:, 0:128], 7, None, A.bitwise_and))
+    v(V.tensor_scalar(T.m8[:], T.c256[:, 0:128], 3, None, A.arith_shift_right))
+    v(V.tensor_scalar(T.m15[:], T.c256[:, 0:128], 15, None, A.bitwise_and))
+    v(V.tensor_copy(T.kf[:, 0:1], T.kk[:, 0:1]))
+    v(V.memset(T.Mone[:], SC))
+    v(V.memset(T.S[:, 0:1], -Q * r / 128.0 - 7.5 / 128.0))
+    if zeros:
+        v(V.memset(T.win[:, w1:w1 + 4], 0.0))
+    vw(nv[0])
+    v(V.tensor_copy(T.kf[:, 1:2], T.k7[:, 0:1]))
+    v(V.tensor_copy(T.kf[:, 2:3], T.k8[:, 0:1]))
+    v(V.tensor_scalar(T.kf[:, 3:4], T.kf[:, 0:1], 15.0, None, A.is_equal))
+    v(V.tensor_scalar(T.I16[:], T.c256[:, 0:128], T.kf[:, 0:1], None, A.is_equal))
+    v(V.tensor_scalar(T.ilo[:], T.m15[:], -7.0, SC, A.add, A.mult))
+    vw(nv[0])
+    v(V.tensor_scalar(T.Meq[:], T.m7[:], T.kf[:, 1:2], SC, A.is_equal, A.mult))
+    v(V.tensor_scalar(T.Mlt[:], T.m7[:], T.kf[:, 1:2], SC, A.is_gt, A.mult))
+    v(V.tensor_scalar(T.Mgt[:], T.m7[:], T.kf[:, 1:2], SC, A.is_lt, A.mult))
+    v(V.tensor_scalar(T.M3a[:], T.m8[:], T.kf[:, 2:3], -1.0, A.is_lt, A.mult))
+    v(V.tensor_scalar(T.S2[:], T.I16[:], -1.0, T.kf[:, 3:4], A.mult, A.add))
+    v(V.memset(T.Cn[:, 0:1], -64.0 * nt))
+    vw(nv[0])
+    v(V.tensor_tensor(T.M3[:], T.M3a[:], T.Meq[:], A.mult))
+    v(V.tensor_copy(T.Sca[:, 0:1], T.Cn[:, 0:1]))
+
+    S.wait_ge(sem.v, a_ihi)
+    a_ones = s(S.activation(T.ones[:], T.ihi[:], ActivationFunctionType.Sigmoid, bias=100.0, scale=0.0))
+
+    V.wait_ge(sem.lns, 16)
+    V.wait_ge(sem.near, n_near)
+    vw(v(V.tensor_copy(T.Lf[:, 0:nt], T.L[:, 8 * first:8 * first + nt])))
+    V.wait_ge(sem.s, a_ones)
+    a_scan = v(V.tensor_tensor_scan(T.S[:, 1:1 + nt], T.ones[:, 0:nt], T.Lf[:, 0:nt],
+                                    -Q * r / 128.0 - 7.5 / 128.0, A.mult, A.add))
+    P.wait_ge(sem.v, a_scan)
+    P.matmul(T.psB[:, 0:nl], T.Mlt[:], T.S[:, 8:8 * nl + 1:8], True, False)
+    pe(P.matmul(T.psB[:, 0:nl], T.Mgt[:], T.S[:, 0:8 * nl - 7:8], False, True))
+    P.matmul(T.psP[:, 0:nt], T.Meq[:], T.S[:, 1:1 + nt], True, False)
+    a_near = pe(P.matmul(T.psP[:, 0:nt], T.M3[:], T.Lf[:, 0:nt], False, True))
+    V.wait_ge(sem.pe, a_near)
+    for l in range(nl):
+        v(V.tensor_scalar(T.Xn[:, 8 * l:8 * l + 8], T.psP[:, 8 * l:8 * l + 8], T.psB[:, l:l + 1], None, A.add))
+
+    if nfar:
+        Y.wait_ge(sem.farm, n_far)
+        Y.dma_start(T.FL[:, 0:8 * nfar], T.far[0:nfar]).then_inc(sem.fl, 16)
+        V.wait_ge(sem.fl, 16)
+        vw(v(V.tensor_copy(T.FLf[:, 0:8 * nfar], T.FL[:, 0:8 * nfar])))
+        a_fr = v(V.tensor_reduce(T.fr[:, 0:1], T.FLf[:, 0:8 * nfar], AxisListType.X, A.add))
+        P.wait_ge(sem.v, a_fr)
+        V.wait_ge(sem.pe, pe(P.matmul(T.psF[:, 0:1], T.Mone[:], T.fr[:, 0:1], True, True)))
+        vw(nv[0])
+        vw(v(V.tensor_scalar(T.X[:, 0:nt], T.Xn[:, 0:nt], T.psF[:, 0:1], -7.5 * SC, A.add, A.max)))
+    else:
+        vw(nv[0])
+        vw(v(V.tensor_scalar(T.X[:, 0:nt], T.Xn[:, 0:nt], -7.5 * SC, None, A.max)))
+    vw(v(V.tensor_scalar(T.hi[:, 0:nt], T.X[:, 0:nt], MAGIC, MAGIC, A.add, A.subtract)))
+    a_d = v(V.tensor_tensor(T.dd[:, 0:nt], T.hi[:, 0:nt], T.X[:, 0:nt], A.subtract))
+
+    S.wait_ge(sem.v, a_d)
+    for t in range(nt):
+        a_v = v(V.tensor_scalar(T.rhs[:, 256 * t:256 * t + 256], T.ihi[:], T.hi[:, t:t + 1], None, A.is_equal))
+        a_s = s(S.activation(T.lhs[:, 128 * t:128 * t + 128], T.ilo[:], ActivationFunctionType.Sigmoid,
+                             bias=T.dd[:, t:t + 1], scale=1.0))
+        P.wait_ge(sem.v, a_v)
+        P.wait_ge(sem.s, a_s)
+        ins = P.matmul(T.psA[:, 0:256], T.lhs[:, 128 * t:128 * t + 128], T.rhs[:, 256 * t:256 * t + 256],
+                       t == 0, t == nt - 1)
+        if t == nt - 1:
+            V.wait_ge(sem.pe, pe(ins))
+
+    a_sc = v(V.tensor_tensor_scan(T.Sca[:, 1:257], T.ones[:], T.psA[:, 0:256], -64.0 * nt, A.mult, A.add))
+    P.wait_ge(sem.v, a_sc)
+    P.matmul(T.psI[:, 0:256], T.I16[:], T.Sca[:, 1:257], True, False)
+    V.wait_ge(sem.pe, pe(P.matmul(T.psI[:, 0:256], T.S2[:], T.Sca[:, 0:256], False, True)))
+    a_o1 = v(V.tensor_scalar(T.offs[:, 0:96], T.psI[:, 0:96], 64.0 * nt, None, A.add))
+
+    win = T.win[:, w0:w1 + (4 if zeros else 0)]
+    for eng in (V, S):
+        eng.wait_ge(sem.xa, 16)
+        eng.wait_ge(sem.xb, 16)
+        eng.wait_ge(sem.xl, n_x)
+    vw(a_o1)
+    S.wait_ge(sem.v, a_o1)
+    pieces, q0 = [], 0
+    for k, w in enumerate((256, 256, 512, 512, 768, 768, 512, 512)):
+        q1 = q0 + w
+        src = win.indirect(T.offs[:, q0 // 16:q1 // 16])
+        if k == 2:
+            a_o2 = v(V.tensor_scalar(T.offs[:, 96:256], T.psI[:, 96:256], 64.0 * nt, None, A.add))
+        if k in (4, 5):
+            (V, S)[k & 1].wait_ge(sem.v, a_o2)
+        if k & 1:
+            a = s(S.activation(T.yb[:, q0:q1], src, ActivationFunctionType.Copy))
+        else:
+            a = v(V.tensor_copy(T.yb[:, q0:q1], src))
+        pieces.append((k, a, q0, q1))
+        q0 = q1
+    n_y = n_s = 0
+    for k, a, q0, q1 in pieces:
+        if k in (5, 7):
+            S.wait_ge(sem.s, a)
+            S.dma_start(T.y[:, q0:q1], T.yb[:, q0:q1]).then_inc(sem.sts, 16)
+            n_s += 16
+        else:
+            Y.wait_ge(sem.s if k & 1 else sem.v, a)
+            Y.dma_start(T.y[:, q0:q1], T.yb[:, q0:q1]).then_inc(sem.sty, 16)
+            n_y += 16
+
+    for name, n in (("near", n_near), ("farm", n_far), ("hpl", n_hp), ("xl", n_x), ("ls", sent[0]), ("lns", 16),
+                    ("xa", 16), ("xb", 16), ("fl", 16 if nfar else 0), ("gi", 2), ("v", nv[0]), ("s", ns[0]),
+                    ("pe", npe[0]), ("sty", n_y), ("sts", n_s)):
+        if n:
+            g.wait_ge(sem[name], n)

@@ -2,56 +2,25 @@ from concourse.bass import DstId, RemoteDMATransfer
 from concourse.mybir import AluOpType, AxisListType, ActivationFunctionType
 
 N, J, Q, CORES_ALL = 12, 1024, 4096, 256
+W = 64
+HALF = (W - 1) / 2.0
 SC = 256.0
-MAGIC = 1.5 * 2.0 ** 35
+MAGIC = 1.5 * 2.0 ** 37
 
-SCRATCH = {
-    "dln": ("dram", [128, 8], "int32"),
-    "hp": ("dram", [128, 8], "int32"),
-    "far": ("dram", [10, 128, 8], "int32"),
-    "L": ("sbuf", [128, 24], "int32"),
-    "Lf": ("sbuf", [128, 24], "float32"),
-    "FL": ("sbuf", [128, 80], "int32"),
-    "FLf": ("sbuf", [128, 80], "float32"),
-    "fr": ("sbuf", [128, 4], "float32"),
-    "S": ("sbuf", [128, 32], "float32"),
-    "win": ("sbuf", [128, 3076], "float32"),
-    "hb": ("sbuf", [128, 512], "float32"),
-    "yb": ("sbuf", [128, 4096], "float32"),
-    "c256": ("sbuf", [128, 256], "int32"),
-    "kk": ("sbuf", [128, 4], "int32"),
-    "k7": ("sbuf", [128, 4], "int32"),
-    "k8": ("sbuf", [128, 4], "int32"),
-    "m7": ("sbuf", [128, 128], "int32"),
-    "m8": ("sbuf", [128, 128], "int32"),
-    "m15": ("sbuf", [128, 128], "int32"),
-    "kf": ("sbuf", [128, 4], "float32"),
-    "Meq": ("sbuf", [128, 128], "float32"),
-    "Mlt": ("sbuf", [128, 128], "float32"),
-    "Mgt": ("sbuf", [128, 128], "float32"),
-    "M3a": ("sbuf", [128, 128], "float32"),
-    "M3": ("sbuf", [128, 128], "float32"),
-    "Mone": ("sbuf", [128, 128], "float32"),
-    "ihi": ("sbuf", [128, 256], "bfloat16"),
-    "ilo": ("sbuf", [128, 128], "bfloat16"),
-    "ones": ("sbuf", [128, 256], "bfloat16"),
-    "I16": ("sbuf", [128, 128], "float16"),
-    "S2": ("sbuf", [128, 128], "float16"),
-    "rhs": ("sbuf", [128, 24 * 256], "bfloat16"),
-    "lhs": ("sbuf", [128, 24 * 128], "bfloat16"),
-    "Xn": ("sbuf", [128, 24], "float32"),
-    "X": ("sbuf", [128, 24], "float32"),
-    "hi": ("sbuf", [128, 24], "float32"),
-    "dd": ("sbuf", [128, 24], "float32"),
-    "Cn": ("sbuf", [128, 4], "float32"),
-    "Sca": ("sbuf", [128, 264], "float16"),
-    "offs": ("sbuf", [128, 256], "uint16"),
-    "psP": ("psum", [128, 512], "float32"),
-    "psB": ("psum", [128, 512], "float32"),
-    "psF": ("psum", [128, 512], "float32"),
-    "psA": ("psum", [128, 512], "float32"),
-    "psI": ("psum", [128, 512], "float32"),
-}
+SCRATCH = {"dln": ("dram", [128, 8], "int32"), "hp": ("dram", [128, 8], "int32"), "far": ("dram", [10, 128, 8], "int32")}
+for _n, _w, _d in (("L", 24, "int32"), ("Lf", 24, "float32"), ("FL", 80, "int32"), ("FLf", 80, "float32"),
+                   ("fr", 4, "float32"), ("S", 32, "float32"), ("win", 3076, "float32"), ("hb", 512, "float32"),
+                   ("yb", 4096, "float32"), ("c128", 128, "int32"), ("kk", 4, "int32"), ("k7", 4, "int32"),
+                   ("k8", 4, "int32"), ("m7", 128, "int32"), ("m8", 128, "int32"), ("m15", 128, "int32"),
+                   ("kf", 12, "float32"), ("Meq", 128, "float32"), ("Mlt", 128, "float32"), ("Mgt", 128, "float32"),
+                   ("M3a", 128, "float32"), ("M3", 128, "float32"), ("Mone", 128, "float32"), ("ihi", W, "bfloat16"),
+                   ("ilo", W, "bfloat16"), ("ones", W, "bfloat16"), ("G", 512, "float16"), ("H", 512, "float16"),
+                   ("rhs", 24 * W, "bfloat16"), ("lhs", 24 * W, "bfloat16"), ("Xn", 24, "float32"),
+                   ("X", 24, "float32"), ("hi", 24, "float32"), ("dd", 24, "float32"), ("Cn", 4, "float32"),
+                   ("Sca", 80, "float16"), ("offs", 256, "uint16")):
+    SCRATCH[_n] = ("sbuf", [128, _w], _d)
+for _n in ("psP", "psB", "psF", "psA", "psI"):
+    SCRATCH[_n] = ("psum", [128, 512], "float32")
 SEMAPHORES = ["lnd", "lns", "xa", "xb", "near", "hpl", "farm", "fl", "xl", "hx0", "hx1", "ls", "gi", "v", "s", "pe",
               "sty", "sts"]
 
@@ -76,26 +45,22 @@ def helpers(q, T, topo):
 def list_calls(q, T, topo):
     c = T.cores[q]
     if q % 2 == 0:
-        a, b = split(topo.mask(c, T.cores[q + 1]), 2)
-        return [[("dln", [q + 1], ("hp", 0), a), ("dln", [q + 1], ("L", 0), b)], []]
+        p = split(topo.mask(c, T.cores[q + 1]), 8)
+        return [[("dln", [q + 1], ("hp", 0), p[0]), ("dln", [q + 1], ("L", 0), p[1] | p[2])], []]
     on = topo.mask(c, T.cores[q - 1])
+    off = topo.mask(c, T.cores[q + 1 if q + 1 < N else q - 2])
+    lo, up = split(off, 2)
     first, second = [], []
     mine, his = list(range(q + 2, N)), list(range(q + 1, N))
     if q + 1 < N:
-        off = topo.mask(c, T.cores[q + 1])
-        parts = split(off, 2) if mine else [off]
-        first.append(("dln", [q + 1], ("L", 0), parts[0]))
-        if mine:
-            first.append(("dln", mine, ("far", q), parts[1]))
-        first.append(("dln", [q - 1], ("L", 16), on & ~off))
-    else:
-        first.append(("dln", [q - 1], ("L", 16), on))
-    off = topo.mask(c, T.cores[q + 1] if q + 1 < N else T.cores[q - 2])
-    parts = split(off, 2) if (his and q >= 3) else [off, off]
+        first.append(("dln", [q + 1], ("L", 0), lo))
+    if mine:
+        first.append(("dln", mine, ("far", q), up))
+    first.append(("dln", [q - 1], ("L", 16), split(on & ~off, 2)[0]))
     if his:
-        second.append(("hp", his, ("far", q - 1), parts[0]))
+        second.append(("hp", his, ("far", q - 1), up))
     if q >= 3:
-        second.append(("hp", [q - 2], ("L", 16), parts[1]))
+        second.append(("hp", [q - 2], ("L", 16), lo))
     return [first, second]
 
 
@@ -175,8 +140,10 @@ def rank_program(g, core, T, topo):
     first, last = (1 if r == 0 else 0), (1 if r == N - 1 else 2)
     nl = last - first + 1
     nt = 8 * nl
+    mid = 64.0 * nt
     w0, w1 = first * J, (last + 1) * J
     zeros = r >= N - 2
+    init = (-Q * r - HALF) / 128.0
     V, S, P, Y = g.vector, g.scalar, g.tensor, g.sync
     A = AluOpType
     nfar = max(0, r - 1)
@@ -187,7 +154,7 @@ def rank_program(g, core, T, topo):
     Y.dma_start(T.win[:, J:J + h], T.x[:, 0:h]).then_inc(sem.xa, 16)
     S.dma_start(T.win[:, J + h:2 * J], T.x[:, h:J]).then_inc(sem.xb, 16)
 
-    g.iota(T.c256[:], [[1, 256]], 0, 0).then_inc(sem.gi, 1)
+    g.iota(T.c128[:], [[1, 128]], 0, 0).then_inc(sem.gi, 1)
     g.iota(T.kk[:, 0:1], [[1, 1]], 0, 1).then_inc(sem.gi, 1)
     g.wait_ge(sem.lnd, 16)
     for k, call in enumerate(list_calls(r, T, topo)):
@@ -233,34 +200,35 @@ def rank_program(g, core, T, topo):
         V.wait_ge(sem.v, n)
 
     V.wait_ge(sem.gi, 2)
-    v(V.tensor_scalar(T.ihi[:], T.c256[:], 16.0 * SC, None, A.mult))
-    a_ihi = nv[0]
+    a_ihi = v(V.tensor_scalar(T.ihi[:], T.c128[:, 0:W], W * SC, None, A.mult))
     v(V.tensor_scalar(T.k7[:, 0:1], T.kk[:, 0:1], 7, None, A.bitwise_and))
     v(V.tensor_scalar(T.k8[:, 0:1], T.kk[:, 0:1], 3, None, A.arith_shift_right))
-    v(V.tensor_scalar(T.m7[:], T.c256[:, 0:128], 7, None, A.bitwise_and))
-    v(V.tensor_scalar(T.m8[:], T.c256[:, 0:128], 3, None, A.arith_shift_right))
-    v(V.tensor_scalar(T.m15[:], T.c256[:, 0:128], 15, None, A.bitwise_and))
-    v(V.tensor_copy(T.kf[:, 0:1], T.kk[:, 0:1]))
+    v(V.tensor_scalar(T.m7[:], T.c128[:], 7, None, A.bitwise_and))
+    v(V.tensor_scalar(T.m8[:], T.c128[:], 3, None, A.arith_shift_right))
+    v(V.tensor_scalar(T.m15[:], T.c128[:], 15, None, A.bitwise_and))
+    for a in range(4):
+        v(V.tensor_scalar(T.kf[:, 4 + a:5 + a], T.kk[:, 0:1], -16.0 * a, None, A.add))
+    v(V.tensor_scalar(T.kf[:, 3:4], T.kk[:, 0:1], W - 1.0, None, A.is_equal))
     v(V.memset(T.Mone[:], SC))
-    v(V.memset(T.S[:, 0:1], -Q * r / 128.0 - 7.5 / 128.0))
+    v(V.memset(T.S[:, 0:1], init))
+    v(V.memset(T.Cn[:, 0:1], -mid))
+    v(V.tensor_scalar(T.ilo[:], T.c128[:, 0:W], 0.5 - HALF, SC, A.add, A.mult))
     if zeros:
         v(V.memset(T.win[:, w1:w1 + 4], 0.0))
     vw(nv[0])
     v(V.tensor_copy(T.kf[:, 1:2], T.k7[:, 0:1]))
     v(V.tensor_copy(T.kf[:, 2:3], T.k8[:, 0:1]))
-    v(V.tensor_scalar(T.kf[:, 3:4], T.kf[:, 0:1], 15.0, None, A.is_equal))
-    v(V.tensor_scalar(T.I16[:], T.c256[:, 0:128], T.kf[:, 0:1], None, A.is_equal))
-    v(V.tensor_scalar(T.ilo[:], T.m15[:], -7.0, SC, A.add, A.mult))
+    v(V.tensor_copy(T.Sca[:, 0:1], T.Cn[:, 0:1]))
+    for a in range(4):
+        v(V.tensor_scalar(T.G[0:W, 128 * a:128 * a + 128], T.m15[0:W, :], T.kf[0:W, 4 + a:5 + a], None, A.is_equal))
     vw(nv[0])
     v(V.tensor_scalar(T.Meq[:], T.m7[:], T.kf[:, 1:2], SC, A.is_equal, A.mult))
+    v(V.tensor_scalar(T.M3a[:], T.m8[:], T.kf[:, 2:3], -1.0, A.is_lt, A.mult))
     v(V.tensor_scalar(T.Mlt[:], T.m7[:], T.kf[:, 1:2], SC, A.is_gt, A.mult))
     v(V.tensor_scalar(T.Mgt[:], T.m7[:], T.kf[:, 1:2], SC, A.is_lt, A.mult))
-    v(V.tensor_scalar(T.M3a[:], T.m8[:], T.kf[:, 2:3], -1.0, A.is_lt, A.mult))
-    v(V.tensor_scalar(T.S2[:], T.I16[:], -1.0, T.kf[:, 3:4], A.mult, A.add))
-    v(V.memset(T.Cn[:, 0:1], -64.0 * nt))
+    v(V.tensor_scalar(T.H[0:W, :], T.G[0:W, :], -1.0, T.kf[0:W, 3:4], A.mult, A.add))
     vw(nv[0])
     v(V.tensor_tensor(T.M3[:], T.M3a[:], T.Meq[:], A.mult))
-    v(V.tensor_copy(T.Sca[:, 0:1], T.Cn[:, 0:1]))
 
     S.wait_ge(sem.v, a_ihi)
     a_ones = s(S.activation(T.ones[:], T.ihi[:], ActivationFunctionType.Sigmoid, bias=100.0, scale=0.0))
@@ -269,8 +237,7 @@ def rank_program(g, core, T, topo):
     V.wait_ge(sem.near, n_near)
     vw(v(V.tensor_copy(T.Lf[:, 0:nt], T.L[:, 8 * first:8 * first + nt])))
     V.wait_ge(sem.s, a_ones)
-    a_scan = v(V.tensor_tensor_scan(T.S[:, 1:1 + nt], T.ones[:, 0:nt], T.Lf[:, 0:nt],
-                                    -Q * r / 128.0 - 7.5 / 128.0, A.mult, A.add))
+    a_scan = v(V.tensor_tensor_scan(T.S[:, 1:1 + nt], T.ones[:, 0:nt], T.Lf[:, 0:nt], init, A.mult, A.add))
     P.wait_ge(sem.v, a_scan)
     P.matmul(T.psB[:, 0:nl], T.Mlt[:], T.S[:, 8:8 * nl + 1:8], True, False)
     pe(P.matmul(T.psB[:, 0:nl], T.Mgt[:], T.S[:, 0:8 * nl - 7:8], False, True))
@@ -289,30 +256,32 @@ def rank_program(g, core, T, topo):
         P.wait_ge(sem.v, a_fr)
         V.wait_ge(sem.pe, pe(P.matmul(T.psF[:, 0:1], T.Mone[:], T.fr[:, 0:1], True, True)))
         vw(nv[0])
-        vw(v(V.tensor_scalar(T.X[:, 0:nt], T.Xn[:, 0:nt], T.psF[:, 0:1], -7.5 * SC, A.add, A.max)))
+        vw(v(V.tensor_scalar(T.X[:, 0:nt], T.Xn[:, 0:nt], T.psF[:, 0:1], -HALF * SC, A.add, A.max)))
     else:
         vw(nv[0])
-        vw(v(V.tensor_scalar(T.X[:, 0:nt], T.Xn[:, 0:nt], -7.5 * SC, None, A.max)))
+        vw(v(V.tensor_scalar(T.X[:, 0:nt], T.Xn[:, 0:nt], -HALF * SC, None, A.max)))
     vw(v(V.tensor_scalar(T.hi[:, 0:nt], T.X[:, 0:nt], MAGIC, MAGIC, A.add, A.subtract)))
     a_d = v(V.tensor_tensor(T.dd[:, 0:nt], T.hi[:, 0:nt], T.X[:, 0:nt], A.subtract))
 
     S.wait_ge(sem.v, a_d)
     for t in range(nt):
-        a_v = v(V.tensor_scalar(T.rhs[:, 256 * t:256 * t + 256], T.ihi[:], T.hi[:, t:t + 1], None, A.is_equal))
-        a_s = s(S.activation(T.lhs[:, 128 * t:128 * t + 128], T.ilo[:], ActivationFunctionType.Sigmoid,
-                             bias=T.dd[:, t:t + 1], scale=1.0))
+        b = slice(W * t, W * t + W)
+        a_v = v(V.tensor_scalar(T.rhs[:, b], T.ihi[:], T.hi[:, t:t + 1], None, A.is_ge))
+        a_s = s(S.activation(T.lhs[:, b], T.ilo[:], ActivationFunctionType.Sigmoid, bias=T.dd[:, t:t + 1], scale=1.0))
         P.wait_ge(sem.v, a_v)
         P.wait_ge(sem.s, a_s)
-        ins = P.matmul(T.psA[:, 0:256], T.lhs[:, 128 * t:128 * t + 128], T.rhs[:, 256 * t:256 * t + 256],
-                       t == 0, t == nt - 1)
+        ins = P.matmul(T.psA[0:W, 0:W], T.lhs[:, b], T.rhs[:, b], t == 0, t == nt - 1)
         if t == nt - 1:
             V.wait_ge(sem.pe, pe(ins))
 
-    a_sc = v(V.tensor_tensor_scan(T.Sca[:, 1:257], T.ones[:], T.psA[:, 0:256], -64.0 * nt, A.mult, A.add))
+    a_sc = v(V.tensor_scalar(T.Sca[0:W, 1:1 + W], T.psA[0:W, 0:W], -mid, None, A.add))
     P.wait_ge(sem.v, a_sc)
-    P.matmul(T.psI[:, 0:256], T.I16[:], T.Sca[:, 1:257], True, False)
-    V.wait_ge(sem.pe, pe(P.matmul(T.psI[:, 0:256], T.S2[:], T.Sca[:, 0:256], False, True)))
-    a_o1 = v(V.tensor_scalar(T.offs[:, 0:96], T.psI[:, 0:96], 64.0 * nt, None, A.add))
+    for a in range(4):
+        b = slice(128 * a, 128 * a + 128)
+        P.matmul(T.psI[:, a:256:4], T.G[0:W, b], T.Sca[0:W, 1:1 + W], True, False)
+        ins = P.matmul(T.psI[:, a:256:4], T.H[0:W, b], T.Sca[0:W, 0:W], False, True)
+    V.wait_ge(sem.pe, pe(ins))
+    a_o1 = v(V.tensor_scalar(T.offs[:, 0:96], T.psI[:, 0:96], mid, None, A.add))
 
     win = T.win[:, w0:w1 + (4 if zeros else 0)]
     for eng in (V, S):
@@ -326,7 +295,7 @@ def rank_program(g, core, T, topo):
         q1 = q0 + w
         src = win.indirect(T.offs[:, q0 // 16:q1 // 16])
         if k == 2:
-            a_o2 = v(V.tensor_scalar(T.offs[:, 96:256], T.psI[:, 96:256], 64.0 * nt, None, A.add))
+            a_o2 = v(V.tensor_scalar(T.offs[:, 96:256], T.psI[:, 96:256], mid, None, A.add))
         if k in (4, 5):
             (V, S)[k & 1].wait_ge(sem.v, a_o2)
         if k & 1:

from concourse.bass import DstId, RemoteDMATransfer
from concourse.mybir import AluOpType, AxisListType, ActivationFunctionType

N, J, Q, CORES_ALL = 12, 1024, 4096, 256
W = 64
HALF = (W - 1) / 2.0
SC = 256.0
MAGIC = 1.5 * 2.0 ** 37

SCRATCH = {"dln": ("dram", [128, 8], "int32"), "hp": ("dram", [128, 8], "int32"), "far": ("dram", [10, 128, 8], "int32")}
for _n, _w, _d in (("L", 24, "int32"), ("Lf", 24, "float32"), ("FL", 80, "int32"), ("FLf", 80, "float32"),
                   ("fr", 4, "float32"), ("S", 32, "float32"), ("win", 3076, "float32"), ("hb", 512, "float32"),
                   ("yb", 4096, "float32"), ("c128", 128, "int32"), ("kk", 4, "int32"), ("k7", 4, "int32"),
                   ("k8", 4, "int32"), ("m7", 128, "int32"), ("m8", 128, "int32"), ("m15", 128, "int32"),
                   ("kf", 12, "float32"), ("Meq", 128, "float32"), ("Mlt", 128, "float32"), ("Mgt", 128, "float32"),
                   ("M3a", 128, "float32"), ("M3", 128, "float32"), ("Mone", 128, "float32"), ("ihi", W, "bfloat16"),
                   ("ilo", W, "bfloat16"), ("ones", W, "bfloat16"), ("G", 512, "float16"), ("H", 512, "float16"),
                   ("rhs", 24 * W, "bfloat16"), ("lhs", 24 * W, "bfloat16"), ("Xn", 24, "float32"),
                   ("X", 24, "float32"), ("hi", 24, "float32"), ("dd", 24, "float32"), ("Cn", 4, "float32"),
                   ("Sca", 80, "float16"), ("offs", 256, "uint16")):
    SCRATCH[_n] = ("sbuf", [128, _w], _d)
for _n in ("psP", "psB", "psF", "psA", "psI"):
    SCRATCH[_n] = ("psum", [128, 512], "float32")
SEMAPHORES = ["lnd", "lns", "xa", "xb", "near", "hpl", "farm", "fl", "xl", "hx0", "hx1", "ls", "gi", "v", "s", "pe",
              "sty", "sts"]


def split(mask, n):
    bits = [1 << b for b in range(16) if mask >> b & 1]
    k = len(bits) // n
    return [sum(bits[i * k:(i + 1) * k]) for i in range(n)]


def pop(mask):
    return bin(mask).count("1")


def helpers(q, T, topo):
    c, d = T.cores[q], T.cores[q - 1]
    got = [h for h in range(CORES_ALL) if topo.host(h) == topo.host(c) and topo.chip(h) == topo.chip(c)
           and topo.die(h) == topo.die(c) and T.rank_of(h) is None and topo.may_write(h, d)]
    return got[:2]


def list_calls(q, T, topo):
    c = T.cores[q]
    if q % 2 == 0:
        p = split(topo.mask(c, T.cores[q + 1]), 8)
        return [[("dln", [q + 1], ("hp", 0), p[0]), ("dln", [q + 1], ("L", 0), p[1] | p[2])], []]
    on = topo.mask(c, T.cores[q - 1])
    off = topo.mask(c, T.cores[q + 1 if q + 1 < N else q - 2])
    lo, up = split(off, 2)
    first, second = [], []
    mine, his = list(range(q + 2, N)), list(range(q + 1, N))
    if q + 1 < N:
        first.append(("dln", [q + 1], ("L", 0), lo))
    if mine:
        first.append(("dln", mine, ("far", q), up))
    first.append(("dln", [q - 1], ("L", 16), split(on & ~off, 2)[0]))
    if his:
        second.append(("hp", his, ("far", q - 1), up))
    if q >= 3:
        second.append(("hp", [q - 2], ("L", 16), lo))
    return [first, second]


def x_calls(q, T, topo):
    c = T.cores[q]
    h = J // 2
    mate = q + 1 if q % 2 == 0 else q - 1
    other = q - 1 if q % 2 == 0 else q + 1
    on = topo.mask(c, T.cores[mate])

    def to(d, s0, w, m):
        return (T.cores[d], "win", (q - d + 1) * J + s0, s0, w, m, "xl")
    if not 0 <= other < N:
        return [(h, [to(mate, 0, h, on)]), (J, [to(mate, h, h, on)])]
    if topo.may_write(c, T.cores[other]):
        off = topo.mask(c, T.cores[other])
        return [(s + h, [to(other, s, h, off), to(mate, s, h, on & ~off)]) for s in (0, h)]
    hs = helpers(q, T, topo)
    w = h // 2
    masks = split(topo.mask(c, hs[0]) & topo.mask(c, hs[1]), 2)
    calls = [((a + 1) * h, [(hs[i], "hb", a * w, a * h + i * w, w, masks[i], "hx%d" % a) for i in (0, 1)])
             for a in (0, 1)]
    return calls + [(J, [to(mate, 0, J, on)])]


def rank_program(g, core, T, topo):
    rank = T.rank_of(core)
    sem = T.sem
    sent = [0]

    def fused(transfers):
        out = []
        for src, dsts, mask, rsem in transfers:
            ids = []
            for d, ap in dsts:
                rid, pid = topo.addr(d, core)
                ids.append(DstId(rid=rid, pnc=pid))
            out.append(RemoteDMATransfer(dst_ids=ids, dma_engine_mask=mask, remote_sem=rsem, srcs=[src],
                                         dsts=[ap for d, ap in dsts]))
            sent[0] += pop(mask)
        g.remote_dma_fused(out, local_sem=sem.ls)

    if rank is None:
        for q in range(2, N, 2):
            if topo.may_write(T.cores[q], T.cores[q - 1]):
                continue
            hs = helpers(q, T, topo)
            if core not in hs:
                continue
            i, d, w = hs.index(core), T.cores[q - 1], J // 4
            for a in (0, 1):
                inc = pop(split(topo.mask(T.cores[q], hs[0]) & topo.mask(T.cores[q], hs[1]), 2)[i])
                g.wait_ge(sem["hx%d" % a], inc)
                c0 = 2 * J + a * (J // 2) + i * w
                fused([(T.hb[:, a * w:(a + 1) * w], [(d, T.win[:, c0:c0 + w])], topo.mask(core, d), sem.xl)])
            g.wait_ge(sem.ls, sent[0])
        return

    r = rank
    n_near = n_far = n_hp = n_x = 0
    for q in range(N):
        for call in list_calls(q, T, topo):
            for src, dsts, place, mask in call:
                if r in dsts:
                    n_near += pop(mask) if place[0] == "L" else 0
                    n_far += pop(mask) if place[0] == "far" else 0
                    n_hp += pop(mask) if place[0] == "hp" else 0
        if q == r:
            continue
        for need, call in x_calls(q, T, topo):
            for dst, buf, d0, s0, w, mask, sname in call:
                if dst == core:
                    n_x += pop(mask)
        if q == r + 1 and q % 2 == 0 and not topo.may_write(T.cores[q], core):
            n_x += sum(2 * pop(topo.mask(h, core)) for h in helpers(q, T, topo))

    first, last = (1 if r == 0 else 0), (1 if r == N - 1 else 2)
    nl = last - first + 1
    nt = 8 * nl
    mid = 64.0 * nt
    w0, w1 = first * J, (last + 1) * J
    zeros = r >= N - 2
    init = (-Q * r - HALF) / 128.0
    V, S, P, Y = g.vector, g.scalar, g.tensor, g.sync
    A = AluOpType
    nfar = max(0, r - 1)

    h = J // 2
    Y.dma_start(T.dln[:], T.ln[:]).then_inc(sem.lnd, 16)
    S.dma_start(T.L[:, 8:16], T.ln[:]).then_inc(sem.lns, 16)
    Y.dma_start(T.win[:, J:J + h], T.x[:, 0:h]).then_inc(sem.xa, 16)
    S.dma_start(T.win[:, J + h:2 * J], T.x[:, h:J]).then_inc(sem.xb, 16)

    g.iota(T.c128[:], [[1, 128]], 0, 0).then_inc(sem.gi, 1)
    g.iota(T.kk[:, 0:1], [[1, 1]], 0, 1).then_inc(sem.gi, 1)
    g.wait_ge(sem.lnd, 16)
    for k, call in enumerate(list_calls(r, T, topo)):
        if not call:
            continue
        if k == 1:
            g.wait_ge(sem.hpl, n_hp)
        trs = []
        for src, dsts, place, mask in call:
            if place[0] == "L":
                ap, rs = T.L[:, place[1]:place[1] + 8], sem.near
            elif place[0] == "far":
                ap, rs = T.far[place[1]], sem.farm
            else:
                ap, rs = T.hp[:], sem.hpl
            trs.append((T[src][:], [(T.cores[d], ap) for d in dsts], mask, rs))
        fused(trs)
    for need, call in x_calls(r, T, topo):
        g.wait_ge(sem.xa, 16)
        if need > h:
            g.wait_ge(sem.xb, 16)
        fused([(T.win[:, J + s0:J + s0 + w], [(dst, T[buf][:, d0:d0 + w])], mask, sem[sname])
               for dst, buf, d0, s0, w, mask, sname in call])

    nv, ns, npe = [0], [0], [0]

    def v(ins):
        ins.then_inc(sem.v, 1)
        nv[0] += 1
        return nv[0]

    def s(ins):
        ins.then_inc(sem.s, 1)
        ns[0] += 1
        return ns[0]

    def pe(ins):
        ins.then_inc(sem.pe, 1)
        npe[0] += 1
        return npe[0]

    def vw(n):
        V.wait_ge(sem.v, n)

    V.wait_ge(sem.gi, 2)
    a_ihi = v(V.tensor_scalar(T.ihi[:], T.c128[:, 0:W], W * SC, None, A.mult))
    v(V.tensor_scalar(T.k7[:, 0:1], T.kk[:, 0:1], 7, None, A.bitwise_and))
    v(V.tensor_scalar(T.k8[:, 0:1], T.kk[:, 0:1], 3, None, A.arith_shift_right))
    v(V.tensor_scalar(T.m7[:], T.c128[:], 7, None, A.bitwise_and))
    v(V.tensor_scalar(T.m8[:], T.c128[:], 3, None, A.arith_shift_right))
    v(V.tensor_scalar(T.m15[:], T.c128[:], 15, None, A.bitwise_and))
    for a in range(4):
        v(V.tensor_scalar(T.kf[:, 4 + a:5 + a], T.kk[:, 0:1], -16.0 * a, None, A.add))
    v(V.tensor_scalar(T.kf[:, 3:4], T.kk[:, 0:1], W - 1.0, None, A.is_equal))
    v(V.memset(T.Mone[:], SC))
    v(V.memset(T.S[:, 0:1], init))
    v(V.memset(T.Cn[:, 0:1], -mid))
    v(V.tensor_scalar(T.ilo[:], T.c128[:, 0:W], 0.5 - HALF, SC, A.add, A.mult))
    if zeros:
        v(V.memset(T.win[:, w1:w1 + 4], 0.0))
    vw(nv[0])
    v(V.tensor_copy(T.kf[:, 1:2], T.k7[:, 0:1]))
    v(V.tensor_copy(T.kf[:, 2:3], T.k8[:, 0:1]))
    v(V.tensor_copy(T.Sca[:, 0:1], T.Cn[:, 0:1]))
    for a in range(4):
        v(V.tensor_scalar(T.G[0:W, 128 * a:128 * a + 128], T.m15[0:W, :], T.kf[0:W, 4 + a:5 + a], None, A.is_equal))
    vw(nv[0])
    v(V.tensor_scalar(T.Meq[:], T.m7[:], T.kf[:, 1:2], SC, A.is_equal, A.mult))
    v(V.tensor_scalar(T.M3a[:], T.m8[:], T.kf[:, 2:3], -1.0, A.is_lt, A.mult))
    v(V.tensor_scalar(T.Mlt[:], T.m7[:], T.kf[:, 1:2], SC, A.is_gt, A.mult))
    v(V.tensor_scalar(T.Mgt[:], T.m7[:], T.kf[:, 1:2], SC, A.is_lt, A.mult))
    v(V.tensor_scalar(T.H[0:W, :], T.G[0:W, :], -1.0, T.kf[0:W, 3:4], A.mult, A.add))
    vw(nv[0])
    v(V.tensor_tensor(T.M3[:], T.M3a[:], T.Meq[:], A.mult))

    S.wait_ge(sem.v, a_ihi)
    a_ones = s(S.activation(T.ones[:], T.ihi[:], ActivationFunctionType.Sigmoid, bias=100.0, scale=0.0))

    V.wait_ge(sem.lns, 16)
    V.wait_ge(sem.near, n_near)
    vw(v(V.tensor_copy(T.Lf[:, 0:nt], T.L[:, 8 * first:8 * first + nt])))
    V.wait_ge(sem.s, a_ones)
    a_scan = v(V.tensor_tensor_scan(T.S[:, 1:1 + nt], T.ones[:, 0:nt], T.Lf[:, 0:nt], init, A.mult, A.add))
    P.wait_ge(sem.v, a_scan)
    P.matmul(T.psB[:, 0:nl], T.Mlt[:], T.S[:, 8:8 * nl + 1:8], True, False)
    pe(P.matmul(T.psB[:, 0:nl], T.Mgt[:], T.S[:, 0:8 * nl - 7:8], False, True))
    P.matmul(T.psP[:, 0:nt], T.Meq[:], T.S[:, 1:1 + nt], True, False)
    a_near = pe(P.matmul(T.psP[:, 0:nt], T.M3[:], T.Lf[:, 0:nt], False, True))
    V.wait_ge(sem.pe, a_near)
    for l in range(nl):
        v(V.tensor_scalar(T.Xn[:, 8 * l:8 * l + 8], T.psP[:, 8 * l:8 * l + 8], T.psB[:, l:l + 1], None, A.add))

    if nfar:
        Y.wait_ge(sem.farm, n_far)
        Y.dma_start(T.FL[:, 0:8 * nfar], T.far[0:nfar]).then_inc(sem.fl, 16)
        V.wait_ge(sem.fl, 16)
        vw(v(V.tensor_copy(T.FLf[:, 0:8 * nfar], T.FL[:, 0:8 * nfar])))
        a_fr = v(V.tensor_reduce(T.fr[:, 0:1], T.FLf[:, 0:8 * nfar], AxisListType.X, A.add))
        P.wait_ge(sem.v, a_fr)
        V.wait_ge(sem.pe, pe(P.matmul(T.psF[:, 0:1], T.Mone[:], T.fr[:, 0:1], True, True)))
        vw(nv[0])
        vw(v(V.tensor_scalar(T.X[:, 0:nt], T.Xn[:, 0:nt], T.psF[:, 0:1], -HALF * SC, A.add, A.max)))
    else:
        vw(nv[0])
        vw(v(V.tensor_scalar(T.X[:, 0:nt], T.Xn[:, 0:nt], -HALF * SC, None, A.max)))
    vw(v(V.tensor_scalar(T.hi[:, 0:nt], T.X[:, 0:nt], MAGIC, MAGIC, A.add, A.subtract)))
    a_d = v(V.tensor_tensor(T.dd[:, 0:nt], T.hi[:, 0:nt], T.X[:, 0:nt], A.subtract))

    S.wait_ge(sem.v, a_d)
    for t in range(nt):
        b = slice(W * t, W * t + W)
        a_v = v(V.tensor_scalar(T.rhs[:, b], T.ihi[:], T.hi[:, t:t + 1], None, A.is_ge))
        a_s = s(S.activation(T.lhs[:, b], T.ilo[:], ActivationFunctionType.Sigmoid, bias=T.dd[:, t:t + 1], scale=1.0))
        P.wait_ge(sem.v, a_v)
        P.wait_ge(sem.s, a_s)
        ins = P.matmul(T.psA[0:W, 0:W], T.lhs[:, b], T.rhs[:, b], t == 0, t == nt - 1)
        if t == nt - 1:
            V.wait_ge(sem.pe, pe(ins))

    a_sc = v(V.tensor_scalar(T.Sca[0:W, 1:1 + W], T.psA[0:W, 0:W], -mid, None, A.add))
    P.wait_ge(sem.v, a_sc)
    for a in range(4):
        b = slice(128 * a, 128 * a + 128)
        P.matmul(T.psI[:, a:256:4], T.G[0:W, b], T.Sca[0:W, 1:1 + W], True, False)
        ins = P.matmul(T.psI[:, a:256:4], T.H[0:W, b], T.Sca[0:W, 0:W], False, True)
    V.wait_ge(sem.pe, pe(ins))
    a_o1 = v(V.tensor_scalar(T.offs[:, 0:96], T.psI[:, 0:96], mid, None, A.add))

    win = T.win[:, w0:w1 + (4 if zeros else 0)]
    for eng in (V, S):
        eng.wait_ge(sem.xa, 16)
        eng.wait_ge(sem.xb, 16)
        eng.wait_ge(sem.xl, n_x)
    vw(a_o1)
    S.wait_ge(sem.v, a_o1)
    pieces, q0 = [], 0
    for k, w in enumerate((256, 256, 512, 512, 768, 768, 512, 512)):
        q1 = q0 + w
        src = win.indirect(T.offs[:, q0 // 16:q1 // 16])
        if k == 2:
            a_o2 = v(V.tensor_scalar(T.offs[:, 96:256], T.psI[:, 96:256], mid, None, A.add))
        if k in (4, 5):
            (V, S)[k & 1].wait_ge(sem.v, a_o2)
        if k & 1:
            a = s(S.activation(T.yb[:, q0:q1], src, ActivationFunctionType.Copy))
        else:
            a = v(V.tensor_copy(T.yb[:, q0:q1], src))
        pieces.append((k, a, q0, q1))
        q0 = q1
    n_y = n_s = 0
    for k, a, q0, q1 in pieces:
        if k in (5, 7):
            S.wait_ge(sem.s, a)
            S.dma_start(T.y[:, q0:q1], T.yb[:, q0:q1]).then_inc(sem.sts, 16)
            n_s += 16
        else:
            Y.wait_ge(sem.s if k & 1 else sem.v, a)
            Y.dma_start(T.y[:, q0:q1], T.yb[:, q0:q1]).then_inc(sem.sty, 16)
            n_y += 16

    for name, n in (("near", n_near), ("farm", n_far), ("hpl", n_hp), ("xl", n_x), ("ls", sent[0]), ("lns", 16),
                    ("xa", 16), ("xb", 16), ("fl", 16 if nfar else 0), ("gi", 2), ("v", nv[0]), ("s", ns[0]),
                    ("pe", npe[0]), ("sty", n_y), ("sts", n_s)):
        if n:
            g.wait_ge(sem[name], n)
